import numpy as np
import ml_dtypes

BF16 = ml_dtypes.bfloat16


def bf(x):
    return np.asarray(x, np.float32).astype(BF16)


def f32(x):
    return np.asarray(x, np.float32)


def f64(x):
    return np.asarray(x).astype(np.float64)


def striped(idx):
    return np.tile(idx.reshape(-1, 16).T, (8, 1))


S, K, M, N, E, Q, V, D = 512, 128, 128, 128, 2, 64, 128, 4


def setup_inputs():
    return {"base": bf(np.random.standard_normal((M, S))), "x": bf(np.random.standard_normal((K, N))), "w": bf(1.5 * np.random.standard_normal((E, K, M)) / np.sqrt(K)), "b": f32(0.5 * np.random.standard_normal((M, 1))), "offs": striped(np.random.permutation(S)[:N])}


def reference(base, x, w, b, offs):
    idx = offs[:16].T.reshape(-1)
    z = f64(base).copy()
    for e in range(E):
        z[:, idx[e * Q : (e + 1) * Q]] += f64(w)[e].T @ f64(x)[:, e * Q : (e + 1) * Q]
    z = np.maximum(z + f64(b), 0.0)
    return z.reshape(M, V, D).max(axis=2)

@@ -1,0 +1,55 @@
+import concourse.mybir as mybir
+from concourse.masks import make_identity
+
+F32, BF16, U16 = mybir.dt.float32, mybir.dt.bfloat16, mybir.dt.uint16
+ALU = mybir.AluOpType
+
+FLOPS = 2 * 128 * 128 * 128
+
+
+def tile_rows_unpool_max_relu_kernel(tc, base, x, w, b, offs, out):
+    nc = tc.nc
+    features, cells = base.shape
+    sensors, contraction, width = w.shape
+    points = x.shape[1]
+    pooled = out.shape[1]
+    per_sensor = points // sensors
+    list_columns = per_sensor // 16
+
+    with (
+        tc.tile_pool(name="held", bufs=1) as held,
+        tc.psum_pool(name="psum", bufs=1) as psum,
+    ):
+        base_sb = held.tile([features, cells], BF16, name="base_sb")
+        nc.sync.dma_start(base_sb[:], base)
+        offsets = held.tile([features, points // 16], U16, name="offsets")
+        nc.sync.dma_start(offsets[:], offs)
+        w_sb = held.tile([contraction, sensors, width], BF16, name="w_sb")
+        nc.scalar.dma_start(w_sb[:], w.rearrange("e k m -> k e m"))
+        x_sb = held.tile([contraction, points], BF16, name="x_sb")
+        nc.scalar.dma_start(x_sb[:], x)
+        bias = held.tile([features, 1], F32, name="bias")
+        nc.scalar.dma_start(bias[:], b)
+
+        ident = held.tile([features, features], BF16, name="ident")
+        make_identity(nc, ident[:])
+
+        grid = psum.tile([features, cells], F32, name="grid")
+        nc.tensor.matmul(grid[:], ident[:], base_sb[:], start=True, stop=False)
+
+        for e in range(sensors):
+            nc.tensor.matmul(
+                grid[:].indirect(offsets[:, e * list_columns : (e + 1) * list_columns]),
+                w_sb[:, e, :],
+                x_sb[:, e * per_sensor : (e + 1) * per_sensor],
+                start=False,
+                stop=e == sensors - 1,
+            )
+
+        largest = held.tile([features, pooled], F32, name="largest")
+        nc.vector.tensor_reduce(
+            largest[:], grid[:].rearrange("p (v d) -> p v d", v=pooled), mybir.AxisListType.X, ALU.max
+        )
+        result = held.tile([features, pooled], F32, name="result")
+        nc.vector.tensor_scalar(result[:], largest[:], bias[:, 0:1], 0.0, ALU.add, ALU.max)
+        nc.sync.dma_start(out, result[:])

@@ -25,11 +25,11 @@ def tile_rows_unpool_max_relu_kernel(tc, base, x, w, b, offs, out):
         offsets = held.tile([features, points // 16], U16, name="offsets")
         nc.sync.dma_start(offsets[:], offs)
         w_sb = held.tile([contraction, sensors, width], BF16, name="w_sb")
-        nc.scalar.dma_start(w_sb[:], w.rearrange("e k m -> k e m"))
+        nc.sync.dma_start(w_sb[:], w.rearrange("e k m -> k e m"))
         x_sb = held.tile([contraction, points], BF16, name="x_sb")
-        nc.scalar.dma_start(x_sb[:], x)
+        nc.sync.dma_start(x_sb[:], x)
         bias = held.tile([features, 1], F32, name="bias")
-        nc.scalar.dma_start(bias[:], b)
+        nc.sync.dma_start(bias[:], b)
 
         ident = held.tile([features, features], BF16, name="ident")
         make_identity(nc, ident[:])

import concourse.mybir as mybir
from concourse.masks import make_identity

F32, BF16, U16 = mybir.dt.float32, mybir.dt.bfloat16, mybir.dt.uint16
ALU = mybir.AluOpType

FLOPS = 2 * 128 * 128 * 128


def tile_rows_unpool_max_relu_kernel(tc, base, x, w, b, offs, out):
    nc = tc.nc
    features, cells = base.shape
    sensors, contraction, width = w.shape
    points = x.shape[1]
    pooled = out.shape[1]
    per_sensor = points // sensors
    list_columns = per_sensor // 16

    with (
        tc.tile_pool(name="held", bufs=1) as held,
        tc.psum_pool(name="psum", bufs=1) as psum,
    ):
        base_sb = held.tile([features, cells], BF16, name="base_sb")
        nc.sync.dma_start(base_sb[:], base)
        offsets = held.tile([features, points // 16], U16, name="offsets")
        nc.sync.dma_start(offsets[:], offs)
        w_sb = held.tile([contraction, sensors, width], BF16, name="w_sb")
        nc.sync.dma_start(w_sb[:], w.rearrange("e k m -> k e m"))
        x_sb = held.tile([contraction, points], BF16, name="x_sb")
        nc.sync.dma_start(x_sb[:], x)
        bias = held.tile([features, 1], F32, name="bias")
        nc.sync.dma_start(bias[:], b)

        ident = held.tile([features, features], BF16, name="ident")
        make_identity(nc, ident[:])

        grid = psum.tile([features, cells], F32, name="grid")
        nc.tensor.matmul(grid[:], ident[:], base_sb[:], start=True, stop=False)

        for e in range(sensors):
            nc.tensor.matmul(
                grid[:].indirect(offsets[:, e * list_columns : (e + 1) * list_columns]),
                w_sb[:, e, :],
                x_sb[:, e * per_sensor : (e + 1) * per_sensor],
                start=False,
                stop=e == sensors - 1,
            )

        largest = held.tile([features, pooled], F32, name="largest")
        nc.vector.tensor_reduce(
            largest[:], grid[:].rearrange("p (v d) -> p v d", v=pooled), mybir.AxisListType.X, ALU.max
        )
        result = held.tile([features, pooled], F32, name="result")
        nc.vector.tensor_scalar(result[:], largest[:], bias[:, 0:1], 0.0, ALU.add, ALU.max)
        nc.sync.dma_start(out, result[:])
